import numpy as np
import ml_dtypes

BF16 = ml_dtypes.bfloat16


def bf(x):
    return np.asarray(x, np.float32).astype(BF16)


def f32(x):
    return np.asarray(x, np.float32)


def f64(x):
    return np.asarray(x).astype(np.float64)


def striped(idx):
    return np.concatenate([l.reshape(-1, 16).T for l in idx])


def rows(idx, k):
    return np.tile(np.repeat(idx, 16, axis=0), (k // (16 * 8), 1))


def look(tab, idx):
    return np.take_along_axis(f64(tab), rows(idx, len(tab)), axis=1)


K, S, V, N, M = 512, 2048, 1024, 1024, 128


def setup_inputs():
    return {"tab": f32(np.random.standard_normal((K, S))), "y": f32(np.random.standard_normal((K, V))), "w": bf(np.random.standard_normal((K, M)) / np.sqrt(K)), "b": f32(0.5 * np.random.standard_normal((M, 1))), "offs": striped(np.stack([np.random.permutation(S)[:N] for _ in range(8)]))}


def reference(tab, y, w, b, offs):
    idx = np.stack([g.T.reshape(-1) for g in np.split(offs, 8)])
    t = look(tab, idx)
    x = 1.0 / (1.0 + np.exp(-t)) * f64(y)
    y = f64(w).T @ x
    return np.maximum(y + f64(b), 0.0)

@@ -1,0 +1,55 @@
+import concourse.mybir as mybir
+
+F32, BF16, U16 = mybir.dt.float32, mybir.dt.bfloat16, mybir.dt.uint16
+ACT = mybir.ActivationFunctionType
+ALU = mybir.AluOpType
+
+P = 128
+GROUP = 16
+PIECE = 512
+K, S, N, M = 512, 2048, 1024, 128
+FLOPS = 2 * K * M * N
+
+
+def tile_lookup_gate_sig_relu_kernel(tc, tab, y, w, b, offs, out):
+    nc = tc.nc
+    blocks, pieces = K // P, N // PIECE
+    with (
+        tc.tile_pool(name="sbuf", bufs=1) as sbuf,
+        tc.psum_pool(name="psum", bufs=1) as psum,
+    ):
+        offsets = sbuf.tile([P, N // GROUP], U16, name="offsets")
+        weights = sbuf.tile([P, blocks, M], BF16, name="weights")
+        bias = sbuf.tile([M, 1], F32, name="bias")
+        windows = [sbuf.tile([P, S], F32, name=f"window{k}") for k in range(blocks)]
+        streams = {
+            (k, h): sbuf.tile([P, PIECE], F32, name=f"stream{k}_{h}")
+            for k in range(blocks)
+            for h in range(pieces)
+        }
+
+        nc.sync.dma_start(offsets[:], offs)
+        nc.scalar.dma_start(weights[:], w.rearrange("(k p) m -> p k m", p=P))
+        nc.scalar.dma_start(bias[:], b)
+        for k in range(blocks):
+            nc.sync.dma_start(windows[k][:], tab[k * P : (k + 1) * P, :])
+        for h in range(pieces):
+            for k in range(blocks):
+                nc.sync.dma_start(streams[k, h][:], y[k * P : (k + 1) * P, h * PIECE : (h + 1) * PIECE])
+
+        gates = {}
+        for k in range(blocks):
+            for h in range(pieces):
+                gates[k, h] = sbuf.tile([P, PIECE], F32, name=f"gate{k}_{h}")
+                entries = offsets[:, h * PIECE // GROUP : (h + 1) * PIECE // GROUP]
+                nc.scalar.activation(gates[k, h][:], windows[k][:].indirect(entries), ACT.Sigmoid)
+
+        for h in range(pieces):
+            acc = psum.tile([M, PIECE], F32, name=f"acc{h}")
+            for k in range(blocks):
+                x = sbuf.tile([P, PIECE], BF16, name=f"x{k}_{h}")
+                nc.vector.tensor_tensor(x[:], gates[k, h][:], streams[k, h][:], ALU.mult)
+                nc.tensor.matmul(acc[:], weights[:, k, :], x[:], start=k == 0, stop=k == blocks - 1)
+            result = sbuf.tile([M, PIECE], F32, name=f"result{h}")
+            nc.scalar.activation(result[:], acc[:], ACT.Relu, bias=bias[:])
+            nc.sync.dma_start(out[:, h * PIECE : (h + 1) * PIECE], result[:])

@@ -13,7 +13,10 @@ FLOPS = 2 * K * M * N
 
 def tile_lookup_gate_sig_relu_kernel(tc, tab, y, w, b, offs, out):
     nc = tc.nc
-    blocks, pieces = K // P, N // PIECE
+    blocks = K // P
+    last = blocks - 1
+    pieces = [slice(lo, lo + PIECE) for lo in range(0, N, PIECE)]
+    chunks = [[pieces[0]], [slice(PIECE, PIECE + PIECE // 2), slice(PIECE + PIECE // 2, N)]]
     with (
         tc.tile_pool(name="sbuf", bufs=1) as sbuf,
         tc.psum_pool(name="psum", bufs=1) as psum,
@@ -22,34 +25,45 @@ def tile_lookup_gate_sig_relu_kernel(tc, tab, y, w, b, offs, out):
         weights = sbuf.tile([P, blocks, M], BF16, name="weights")
         bias = sbuf.tile([M, 1], F32, name="bias")
         windows = [sbuf.tile([P, S], F32, name=f"window{k}") for k in range(blocks)]
-        streams = {
-            (k, h): sbuf.tile([P, PIECE], F32, name=f"stream{k}_{h}")
-            for k in range(blocks)
-            for h in range(pieces)
-        }
+        streams = [sbuf.tile([P, N], F32, name=f"stream{k}") for k in range(blocks)]
+        gates = [sbuf.tile([P, N], F32, name=f"gate{k}") for k in range(blocks)]
+        xs = [sbuf.tile([P, N], BF16, name=f"x{k}") for k in range(blocks)]
+        result = sbuf.tile([M, N], F32, name="result")
+
+        warm = sbuf.tile([P, 2], F32, name="warm")
+        nc.vector.memset(warm[:, 0:1], 0.0)
+        nc.scalar.activation(warm[:, 1:2], warm[:, 0:1], ACT.Sigmoid)
+
+        def rows(k):
+            return slice(k * P, (k + 1) * P)
+
+        def cuts(k, h):
+            return chunks[h] if k == last else [pieces[h]]
 
         nc.sync.dma_start(offsets[:], offs)
-        nc.scalar.dma_start(weights[:], w.rearrange("(k p) m -> p k m", p=P))
-        nc.scalar.dma_start(bias[:], b)
-        for k in range(blocks):
-            nc.sync.dma_start(windows[k][:], tab[k * P : (k + 1) * P, :])
-        for h in range(pieces):
-            for k in range(blocks):
-                nc.sync.dma_start(streams[k, h][:], y[k * P : (k + 1) * P, h * PIECE : (h + 1) * PIECE])
+        for k in range(last):
+            nc.sync.dma_start(windows[k][:], tab[rows(k), :])
+        nc.sync.dma_start(weights[:], w.rearrange("(k p) m -> p k m", p=P))
+        nc.sync.dma_start(bias[:], b)
+        nc.sync.dma_start(streams[0][:], y[rows(0), :])
+        nc.sync.dma_start(windows[last][:], tab[rows(last), :])
+        for h in range(len(pieces)):
+            for k in range(1, blocks):
+                for c in cuts(k, h):
+                    nc.sync.dma_start(streams[k][:, c], y[rows(k), c])
 
-        gates = {}
         for k in range(blocks):
-            for h in range(pieces):
-                gates[k, h] = sbuf.tile([P, PIECE], F32, name=f"gate{k}_{h}")
-                entries = offsets[:, h * PIECE // GROUP : (h + 1) * PIECE // GROUP]
-                nc.scalar.activation(gates[k, h][:], windows[k][:].indirect(entries), ACT.Sigmoid)
+            for c in pieces:
+                entries = offsets[:, c.start // GROUP : c.stop // GROUP]
+                nc.scalar.activation(gates[k][:, c], windows[k][:].indirect(entries), ACT.Sigmoid)
 
-        for h in range(pieces):
-            acc = psum.tile([M, PIECE], F32, name=f"acc{h}")
+        for h in range(len(pieces)):
+            accs = [psum.tile([M, c.stop - c.start], F32, name=f"acc{c.start}") for c in chunks[h]]
             for k in range(blocks):
-                x = sbuf.tile([P, PIECE], BF16, name=f"x{k}_{h}")
-                nc.vector.tensor_tensor(x[:], gates[k, h][:], streams[k, h][:], ALU.mult)
-                nc.tensor.matmul(acc[:], weights[:, k, :], x[:], start=k == 0, stop=k == blocks - 1)
-            result = sbuf.tile([M, PIECE], F32, name=f"result{h}")
-            nc.scalar.activation(result[:], acc[:], ACT.Relu, bias=bias[:])
-            nc.sync.dma_start(out[:, h * PIECE : (h + 1) * PIECE], result[:])
+                for c in cuts(k, h):
+                    nc.vector.tensor_tensor(xs[k][:, c], gates[k][:, c], streams[k][:, c], ALU.mult)
+                for acc, c in zip(accs, chunks[h]):
+                    nc.tensor.matmul(acc[:], weights[:, k, :], xs[k][:, c], start=k == 0, stop=k == last)
+            for acc, c in zip(accs, chunks[h]):
+                nc.scalar.activation(result[:, c], acc[:], ACT.Relu, bias=bias[:])
+                nc.sync.dma_start(out[:, c], result[:, c])

import concourse.mybir as mybir

F32, BF16, U16 = mybir.dt.float32, mybir.dt.bfloat16, mybir.dt.uint16
ACT = mybir.ActivationFunctionType
ALU = mybir.AluOpType

P = 128
GROUP = 16
PIECE = 512
K, S, N, M = 512, 2048, 1024, 128
FLOPS = 2 * K * M * N


def tile_lookup_gate_sig_relu_kernel(tc, tab, y, w, b, offs, out):
    nc = tc.nc
    blocks = K // P
    last = blocks - 1
    pieces = [slice(lo, lo + PIECE) for lo in range(0, N, PIECE)]
    chunks = [[pieces[0]], [slice(PIECE, PIECE + PIECE // 2), slice(PIECE + PIECE // 2, N)]]
    with (
        tc.tile_pool(name="sbuf", bufs=1) as sbuf,
        tc.psum_pool(name="psum", bufs=1) as psum,
    ):
        offsets = sbuf.tile([P, N // GROUP], U16, name="offsets")
        weights = sbuf.tile([P, blocks, M], BF16, name="weights")
        bias = sbuf.tile([M, 1], F32, name="bias")
        windows = [sbuf.tile([P, S], F32, name=f"window{k}") for k in range(blocks)]
        streams = [sbuf.tile([P, N], F32, name=f"stream{k}") for k in range(blocks)]
        gates = [sbuf.tile([P, N], F32, name=f"gate{k}") for k in range(blocks)]
        xs = [sbuf.tile([P, N], BF16, name=f"x{k}") for k in range(blocks)]
        result = sbuf.tile([M, N], F32, name="result")

        warm = sbuf.tile([P, 2], F32, name="warm")
        nc.vector.memset(warm[:, 0:1], 0.0)
        nc.scalar.activation(warm[:, 1:2], warm[:, 0:1], ACT.Sigmoid)

        def rows(k):
            return slice(k * P, (k + 1) * P)

        def cuts(k, h):
            return chunks[h] if k == last else [pieces[h]]

        nc.sync.dma_start(offsets[:], offs)
        for k in range(last):
            nc.sync.dma_start(windows[k][:], tab[rows(k), :])
        nc.sync.dma_start(weights[:], w.rearrange("(k p) m -> p k m", p=P))
        nc.sync.dma_start(bias[:], b)
        nc.sync.dma_start(streams[0][:], y[rows(0), :])
        nc.sync.dma_start(windows[last][:], tab[rows(last), :])
        for h in range(len(pieces)):
            for k in range(1, blocks):
                for c in cuts(k, h):
                    nc.sync.dma_start(streams[k][:, c], y[rows(k), c])

        for k in range(blocks):
            for c in pieces:
                entries = offsets[:, c.start // GROUP : c.stop // GROUP]
                nc.scalar.activation(gates[k][:, c], windows[k][:].indirect(entries), ACT.Sigmoid)

        for h in range(len(pieces)):
            accs = [psum.tile([M, c.stop - c.start], F32, name=f"acc{c.start}") for c in chunks[h]]
            for k in range(blocks):
                for c in cuts(k, h):
                    nc.vector.tensor_tensor(xs[k][:, c], gates[k][:, c], streams[k][:, c], ALU.mult)
                for acc, c in zip(accs, chunks[h]):
                    nc.tensor.matmul(acc[:], weights[:, k, :], xs[k][:, c], start=k == 0, stop=k == last)
            for acc, c in zip(accs, chunks[h]):
                nc.scalar.activation(result[:, c], acc[:], ACT.Relu, bias=bias[:])
                nc.sync.dma_start(out[:, c], result[:, c])
